import numpy as np
import ml_dtypes


def mxq(x, axis, fmt="e4m3"):
    dtype, down = {"e4m3": (ml_dtypes.float8_e4m3fn, 7), "e5m2": (ml_dtypes.float8_e5m2, 14)}[fmt]
    v = np.moveaxis(np.asarray(x, np.float32).astype(ml_dtypes.bfloat16).astype(np.float64), axis, -1)
    blocks = v.reshape(v.shape[:-1] + (-1, 32))
    amax = np.abs(blocks).max(-1, keepdims=True)
    byte = np.maximum(np.where(amax > 0, np.frexp(amax)[1] - 1 + 127, 0) - down, 1)
    scale = np.exp2(byte - 127.0)
    codes = (blocks / scale).astype(np.float32).astype(dtype).astype(np.float64)
    return np.moveaxis((codes * scale).reshape(v.shape), -1, axis)


WIDE = False


def mx_kscale(k):
    if not WIDE:
        return np.ones(k)
    levels = np.array([10, -10, 5, -5, 0])
    if k % 512:
        return np.exp2(np.random.permutation(np.resize(levels, k // 32))).repeat(32)
    a = np.empty((k // 512, 16))
    for p in range(k // 512):
        a[p, :8] = np.random.permutation(np.resize(levels, 8))
        for g in range(8):
            far = levels[np.abs(levels - a[p, g]) >= 10]
            a[p, g + 8] = far[np.random.randint(len(far))]
    return np.exp2(a.ravel()).repeat(32)


def f64(x):
    return np.asarray(x).astype(np.float64)


def striped(idx):
    return np.tile(idx.reshape(-1, 16).T, (8, 1)).astype(np.uint16)


def unstriped(offs):
    return offs[:16].T.reshape(-1).astype(np.int64)


def striped8(idx):
    return np.concatenate([x.reshape(-1, 16).T for x in idx]).astype(np.uint16)


def runs(offs, k):
    lists = np.stack([offs[16 * r : 16 * r + 16].T.reshape(-1) for r in range(8)]).astype(np.int64)
    return lists[np.arange(k) % 512 // 64]


def pack_weight(w):
    k, n = w.shape
    w = f64(np.asarray(w, np.float32).astype(ml_dtypes.bfloat16)).reshape(k // 32, 32, n)
    amax = np.abs(w).max(1)
    byte = np.clip(np.where(amax > 0, np.frexp(amax)[1] - 1 + 127 - 7, 1), 1, 254)
    scaled = (w * np.exp2(127.0 - byte)[:, None, :]).reshape(k, n).astype(np.float32)
    words = np.ascontiguousarray(scaled.reshape(k // 512, 128, 4, n).transpose(0, 1, 3, 2)).astype(ml_dtypes.float8_e4m3fn).view(np.uint8)
    return words, np.ascontiguousarray(byte.astype(np.uint8).reshape(k // 512, 16, n))


def unpack_weight(words, scales):
    g, p, n, _ = words.shape
    vals = np.ascontiguousarray(words).view(ml_dtypes.float8_e4m3fn).astype(np.float64) * np.repeat(np.exp2(scales.astype(np.float64) - 127.0), 8, axis=1)[..., None]
    return vals.transpose(0, 1, 3, 2).reshape(g * 512, n)


K, T, S, N, H, W = 512, 2048, 512, 512, 512, 256


def setup_inputs():
    n = np.random.standard_normal
    s = mx_kscale(K)[:, None]
    u = mx_kscale(H)
    packed_xT = pack_weight(n((K, T)) * s)
    perm = np.stack([np.random.permutation(S) for _ in range(8)])
    return {
        "x_words": packed_xT[0],
        "x_scales": packed_xT[1],
        "w1": (n((K, H)) / np.sqrt(K) / s).astype(np.float32),
        "w2": (n((K, H)) / np.sqrt(K) / s).astype(np.float32),
        "gn": (np.random.uniform(0.5, 1.5, (H, 1)) * u[:, None]).astype(np.float32),
        "w3": (n((H, N)) / np.sqrt(H) / u[:, None]).astype(np.float32),
        "offs": striped(np.random.permutation(T)[:S]),
        "hz": striped8(np.random.randint(0, T, (8, S))),
        "n1": striped8(np.stack([np.random.permutation(S) for _ in range(8)])),
        "n2": striped8(np.stack([np.random.permutation(S) for _ in range(8)])),
        "n3": striped8(perm[:, :W]),
        "n4": striped8(perm[:, W:]),
    }


def reference(x_words, x_scales, w1, w2, gn, w3, offs, hz, n1, n2, n3, n4):
    xq = unpack_weight(x_words, x_scales)[:, unstriped(offs)]
    y = mxq(f64(w1), 0, "e4m3").T @ xq
    x_hz = unpack_weight(x_words, x_scales)[np.arange(K)[:, None], runs(hz, K)]
    d = mxq(f64(w2), 0, "e4m3").T @ x_hz
    z = f64(gn) * (0.75 * (y * (d[np.arange(H)[:, None], runs(n2, H)]) - ((y[np.arange(H)[:, None], runs(n1, H)]) * d)))
    h = mxq(f64(w3), 0, "e4m3").T @ mxq(z, 0, "e4m3")
    pa = h[np.arange(N)[:, None], runs(n3, N)]
    pb = h[np.arange(N)[:, None], runs(n4, N)]
    rb = pa - pb
    ra = 0.75 * (pa + pb)
    ds = np.zeros((N, S))
    ds[np.arange(N)[:, None], runs(n3, N)] = ra
    out = ds.copy()
    out[np.arange(N)[:, None], runs(n4, N)] = rb
    return out

@@ -1,0 +1,197 @@
+from contextlib import ExitStack
+
+import concourse.mybir as mybir
+
+K, T, S, N, H, W = 512, 2048, 512, 512, 512, 256
+FLOPS = 2 * S * (2 * K * H + H * N)
+
+F32 = mybir.dt.float32
+BF16 = mybir.dt.bfloat16
+I32 = mybir.dt.int32
+U32 = mybir.dt.uint32
+U16 = mybir.dt.uint16
+U8 = mybir.dt.uint8
+FP8X4 = mybir.dt.float8_e4m3fn_x4
+COPY = mybir.ActivationFunctionType.Copy
+MULT = mybir.AluOpType.mult
+ADD = mybir.AluOpType.add
+SUB = mybir.AluOpType.subtract
+
+P = 128
+PACK = 4
+HALF = 256
+LCOLS = HALF // 16
+
+
+def tile_picked_twhcrossbhaar_none_p_kernel(
+    tc, x_words, x_scales, w1, w2, gn, w3, offs, hz, n1, n2, n3, n4, out
+):
+    nc = tc.nc
+    with ExitStack() as ctx:
+        lists = ctx.enter_context(tc.tile_pool(name="lists", bufs=1))
+        keep = ctx.enter_context(tc.tile_pool(name="keep", bufs=1))
+        psum = ctx.enter_context(tc.psum_pool(name="psum", bufs=1))
+
+        def load_list(src, name):
+            tile = lists.tile(list(src.shape), U16, name=name)
+            nc.sync.dma_start(tile[:], src)
+            return tile
+
+        def load_weight(w, tag):
+            halves = []
+            for c in range(2):
+                raw = keep.tile([P, PACK, HALF], F32, name="raw", tag="%s%d" % (tag, c))
+                nc.sync.dma_start(raw[:], w.rearrange("(p j) c -> p j c", j=PACK)[:, :, c * HALF : (c + 1) * HALF])
+                halves.append(raw)
+            return halves
+
+        def weight_tiles(name):
+            return [keep.tile([P, 2, P, PACK], BF16, name="%s_bf%d" % (name, u), align_bytes=64) for u in range(2)]
+
+        def round_weight(on_scalar, raw, grouped, c, u):
+            src = raw[c][:].rearrange("p j (m u e) -> p u m j e", u=2, e=2)[:, u]
+            dst = grouped[u][:].rearrange("p e m j -> p m j e")[:, c * 64 : (c + 1) * 64]
+            if on_scalar:
+                nc.scalar.activation(dst, src, COPY)
+            else:
+                nc.vector.tensor_copy(dst, src)
+
+        def quantise(src, name):
+            width = src.shape[1] // PACK
+            codes = keep.tile([P, width], U32, name=name + "_codes", align_bytes=64)
+            scales = keep.tile([P, width], U8, name=name + "_scales", align_bytes=64)
+            nc.vector.quantize_mx(out=codes[:].bitcast(FP8X4), scales=scales[:], in_=src)
+            return codes, scales
+
+        def quantise_weight(grouped, u, name):
+            return quantise(grouped[u][:].rearrange("p e m j -> p (e m j)"), "%s_q%d" % (name, u))
+
+        def product(dst, wq, t, codes, scales):
+            w_codes, w_scales = wq[t // 2]
+            cols = slice((t % 2) * P, (t % 2 + 1) * P)
+            nc.tensor.matmul_mx(
+                out=dst,
+                lhsT=w_codes[:, cols].bitcast(FP8X4),
+                lhsT_scale=w_scales[:, cols],
+                rhs=codes[:].bitcast(FP8X4),
+                rhs_scale=scales[:],
+                start=True,
+                stop=True,
+            )
+
+        scale_table = keep.tile([P, T], U8, name="scale_table", align_bytes=64)
+        scale_rows = x_scales[0].bitcast(I32)
+        for q in range(4):
+            nc.sync.dma_start(
+                scale_table[:].bitcast(I32)[32 * q : 32 * (q + 1), :],
+                scale_rows[4 * q : 4 * (q + 1), :].unsqueeze(0).broadcast_to([8, 4, T // 4]),
+            )
+        hz_l = load_list(hz, "hz_l")
+        offs_l = load_list(offs, "offs_l")
+        w1_raw = load_weight(w1, "rawa")
+        word_table = keep.tile([P, T], I32, name="word_table", align_bytes=64)
+        nc.sync.dma_start(word_table[:], x_words[0].rearrange("p c r -> p (c r)").bitcast(I32))
+        w2_raw = load_weight(w2, "rawb")
+        n1_l = load_list(n1, "n1_l")
+        n2_l = load_list(n2, "n2_l")
+        n3_l = load_list(n3, "n3_l")
+        n4_l = load_list(n4, "n4_l")
+        gain = keep.tile([P, PACK], F32, name="gain")
+        nc.gpsimd.dma_start(gain[:], gn.rearrange("(p t) o -> p (t o)", t=PACK))
+
+        hz_picked = keep.tile([P, S], U8, name="hz_picked", align_bytes=64)
+        hz_scales = keep.tile([P, S], U8, name="hz_scales", align_bytes=64)
+        x_scales_picked = keep.tile([P, S], U8, name="x_scales_picked", align_bytes=64)
+        nc.vector.tensor_copy(hz_picked[:], scale_table[:].indirect(hz_l[:]))
+        nc.vector.tensor_copy(x_scales_picked[:], scale_table[:].indirect(offs_l[:]))
+        nc.vector.tensor_copy(hz_scales[:].bitcast(I32), hz_picked[:].bitcast(I32))
+        for a in (2, 3):
+            nc.scalar.dma_start(hz_scales[:].bitcast(I32)[a:P:32, :], hz_picked[:].bitcast(I32)[16 + a : P : 32, :])
+
+        w1_bf = weight_tiles("w1")
+        for c in range(2):
+            for u in range(2):
+                round_weight(True, w1_raw, w1_bf, c, u)
+        w1_q = [quantise_weight(w1_bf, u, "w1") for u in range(2)]
+        w3_raw = load_weight(w3, "rawa")
+
+        x_codes = keep.tile([P, S], U32, name="x_codes", align_bytes=64)
+        hz_codes = keep.tile([P, S], U32, name="hz_codes", align_bytes=64)
+        nc.vector.tensor_copy(x_codes[:], word_table[:].bitcast(U32).indirect(offs_l[:]))
+        nc.vector.tensor_copy(hz_codes[:], word_table[:].bitcast(U32).indirect(hz_l[:]))
+
+        banks = [psum.tile([P, S], F32, name="bank%d" % b) for b in range(8)]
+        for t in range(PACK):
+            product(banks[t][:], w1_q, t, x_codes, x_scales_picked)
+
+        w2_bf = weight_tiles("w2")
+        for c in range(2):
+            for u in range(2):
+                round_weight(c == 0, w2_raw, w2_bf, c, u)
+        w2_q = [quantise_weight(w2_bf, u, "w2") for u in range(2)]
+        for t in range(PACK):
+            product(banks[PACK + t][:], w2_q, t, hz_codes, hz_scales)
+
+        y = [keep.tile([P, S], F32, name="y%d" % t) for t in range(PACK)]
+        d = [keep.tile([P, S], F32, name="d%d" % t) for t in range(PACK)]
+        for t in range(PACK):
+            nc.scalar.activation(y[t][:], banks[t][:], COPY, scale=gain[:, t : t + 1])
+        for t in range(PACK):
+            if t < 2:
+                nc.vector.tensor_scalar(d[t][:], banks[PACK + t][:], 0.75, None, MULT)
+            else:
+                nc.scalar.activation(d[t][:], banks[PACK + t][:], COPY, scale=0.75)
+
+        w3_bf = weight_tiles("w3")
+        for c in range(2):
+            for u in range(2):
+                round_weight(False, w3_raw, w3_bf, c, u)
+        w3_q = [quantise_weight(w3_bf, u, "w3") for u in range(2)]
+
+        z_q = []
+        for c in range(2):
+            cols = slice(c * HALF, (c + 1) * HALF)
+            lcols = slice(c * LCOLS, (c + 1) * LCOLS)
+            first = keep.tile([P, PACK, HALF], F32, name="first%d" % c)
+            second = keep.tile([P, PACK, HALF], F32, name="second%d" % c)
+            for t in range(PACK):
+                y_n1 = keep.tile([P, HALF], F32, name="y_n1_%d_%d" % (c, t))
+                nc.scalar.activation(y_n1[:], y[t][:].indirect(n1_l[:, lcols]), COPY)
+                if c == 0:
+                    nc.vector.tensor_tensor(first[:, t, :], d[t][:].indirect(n2_l[:, lcols]), y[t][:, cols], MULT)
+                else:
+                    d_n2 = keep.tile([P, HALF], F32, name="d_n2_%d" % t)
+                    nc.scalar.activation(d_n2[:], d[t][:].indirect(n2_l[:, lcols]), COPY)
+                    nc.vector.tensor_tensor(first[:, t, :], d_n2[:], y[t][:, cols], MULT)
+                nc.vector.tensor_tensor(second[:, t, :], y_n1[:], d[t][:, cols], MULT)
+            z = keep.tile([P, HALF, PACK], BF16, name="z%d" % c, align_bytes=64)
+            nc.vector.tensor_tensor(
+                z[:].rearrange("p (c e) t -> p c t e", e=2),
+                first[:].rearrange("p t (c e) -> p c t e", e=2),
+                second[:].rearrange("p t (c e) -> p c t e", e=2),
+                SUB,
+            )
+            z_q.append(quantise(z[:].rearrange("p c t -> p (c t)"), "z%d" % c))
+
+        out_rows = out.rearrange("(p t) c -> t p c", t=PACK)
+        for c in range(2):
+            for t in range(PACK):
+                product(banks[t][:, c * HALF : (c + 1) * HALF], w3_q, t, *z_q[c])
+        for t in range(PACK):
+            h = keep.tile([P, S], F32, name="h%d" % t)
+            nc.scalar.activation(h[:], banks[t][:], COPY)
+            a75 = keep.tile([P, W], F32, name="a75_%d" % t)
+            b75 = keep.tile([P, W], F32, name="b75_%d" % t)
+            pa = keep.tile([P, W], F32, name="pa%d" % t)
+            nb = keep.tile([P, W], F32, name="nb%d" % t)
+            res = keep.tile([P, S], F32, name="res%d" % t)
+            if t == 0:
+                nc.vector.tensor_copy(pa[:], h[:].indirect(n3_l[:]))
+            else:
+                nc.scalar.activation(pa[:], h[:].indirect(n3_l[:]), COPY)
+            nc.scalar.activation(nb[:], h[:].indirect(n4_l[:]), COPY, scale=-1.0)
+            nc.scalar.activation(a75[:], pa[:], COPY, scale=0.75)
+            nc.scalar.activation(b75[:], nb[:], COPY, scale=-0.75)
+            nc.vector.tensor_tensor(res[:].indirect(n4_l[:]), pa[:], nb[:], ADD)
+            nc.vector.tensor_tensor(res[:].indirect(n3_l[:]), a75[:], b75[:], ADD)
+            nc.sync.dma_start(out_rows[t], res[:])

@@ -80,22 +80,20 @@ def tile_picked_twhcrossbhaar_none_p_kernel(
             )
 
         scale_table = keep.tile([P, T], U8, name="scale_table", align_bytes=64)
+        table_words = scale_table[:].bitcast(I32)
         scale_rows = x_scales[0].bitcast(I32)
         for q in range(4):
             nc.sync.dma_start(
-                scale_table[:].bitcast(I32)[32 * q : 32 * (q + 1), :],
+                table_words[32 * q : 32 * (q + 1), :],
                 scale_rows[4 * q : 4 * (q + 1), :].unsqueeze(0).broadcast_to([8, 4, T // 4]),
             )
         hz_l = load_list(hz, "hz_l")
         offs_l = load_list(offs, "offs_l")
-        w1_raw = load_weight(w1, "rawa")
+        n1_l = load_list(n1, "n1_l")
         word_table = keep.tile([P, T], I32, name="word_table", align_bytes=64)
         nc.sync.dma_start(word_table[:], x_words[0].rearrange("p c r -> p (c r)").bitcast(I32))
-        w2_raw = load_weight(w2, "rawb")
-        n1_l = load_list(n1, "n1_l")
-        n2_l = load_list(n2, "n2_l")
-        n3_l = load_list(n3, "n3_l")
-        n4_l = load_list(n4, "n4_l")
+        w1_raw = load_weight(w1, "w1_raw")
+        w2_raw = load_weight(w2, "w2_raw")
         gain = keep.tile([P, PACK], F32, name="gain")
         nc.gpsimd.dma_start(gain[:], gn.rearrange("(p t) o -> p (t o)", t=PACK))
 
@@ -106,92 +104,135 @@ def tile_picked_twhcrossbhaar_none_p_kernel(
         nc.vector.tensor_copy(x_scales_picked[:], scale_table[:].indirect(offs_l[:]))
         nc.vector.tensor_copy(hz_scales[:].bitcast(I32), hz_picked[:].bitcast(I32))
         for a in (2, 3):
-            nc.scalar.dma_start(hz_scales[:].bitcast(I32)[a:P:32, :], hz_picked[:].bitcast(I32)[16 + a : P : 32, :])
-
-        w1_bf = weight_tiles("w1")
-        for c in range(2):
-            for u in range(2):
-                round_weight(True, w1_raw, w1_bf, c, u)
-        w1_q = [quantise_weight(w1_bf, u, "w1") for u in range(2)]
-        w3_raw = load_weight(w3, "rawa")
+            nc.sync.dma_start(hz_scales[:].bitcast(I32)[a:P:32, :], hz_picked[:].bitcast(I32)[16 + a : P : 32, :])
+        n2_l = load_list(n2, "n2_l")
+        w3_raw = load_weight(w3, "w3_raw")
+        n3_l = load_list(n3, "n3_l")
+        n4_l = load_list(n4, "n4_l")
 
         x_codes = keep.tile([P, S], U32, name="x_codes", align_bytes=64)
         hz_codes = keep.tile([P, S], U32, name="hz_codes", align_bytes=64)
         nc.vector.tensor_copy(x_codes[:], word_table[:].bitcast(U32).indirect(offs_l[:]))
         nc.vector.tensor_copy(hz_codes[:], word_table[:].bitcast(U32).indirect(hz_l[:]))
 
+        w1_bf = weight_tiles("w1")
+        for c in range(2):
+            for u in range(2):
+                round_weight(True, w1_raw, w1_bf, c, u)
+        w1_q = [quantise_weight(w1_bf, u, "w1") for u in range(2)]
+
         banks = [psum.tile([P, S], F32, name="bank%d" % b) for b in range(8)]
         for t in range(PACK):
             product(banks[t][:], w1_q, t, x_codes, x_scales_picked)
 
-        w2_bf = weight_tiles("w2")
+        w2_bf = weight_tiles("w1")
         for c in range(2):
             for u in range(2):
-                round_weight(c == 0, w2_raw, w2_bf, c, u)
+                round_weight(False, w2_raw, w2_bf, c, u)
         w2_q = [quantise_weight(w2_bf, u, "w2") for u in range(2)]
         for t in range(PACK):
             product(banks[PACK + t][:], w2_q, t, hz_codes, hz_scales)
 
         y = [keep.tile([P, S], F32, name="y%d" % t) for t in range(PACK)]
         d = [keep.tile([P, S], F32, name="d%d" % t) for t in range(PACK)]
-        for t in range(PACK):
-            nc.scalar.activation(y[t][:], banks[t][:], COPY, scale=gain[:, t : t + 1])
-        for t in range(PACK):
-            if t < 2:
-                nc.vector.tensor_scalar(d[t][:], banks[PACK + t][:], 0.75, None, MULT)
+
+        first = [keep.tile([P, PACK, HALF], F32, name="first%d" % c) for c in range(2)]
+        second = [keep.tile([P, PACK, HALF], F32, name="second%d" % c) for c in range(2)]
+        cols = [slice(c * HALF, (c + 1) * HALF) for c in range(2)]
+        lcols = [slice(c * LCOLS, (c + 1) * LCOLS) for c in range(2)]
+
+        def fetch_y(c, t):
+            y_n1 = keep.tile([P, HALF], F32, name="y_n1_%d_%d" % (c, t))
+            nc.scalar.activation(y_n1[:], y[t][:].indirect(n1_l[:, lcols[c]]), COPY)
+            return y_n1
+
+        def second_term(c, t, y_n1):
+            nc.vector.tensor_tensor(second[c][:, t, :], y_n1[:], d[t][:, cols[c]], MULT)
+
+        def first_term(c, t, fused):
+            if fused:
+                nc.vector.tensor_tensor(first[c][:, t, :], d[t][:].indirect(n2_l[:, lcols[c]]), y[t][:, cols[c]], MULT)
             else:
-                nc.scalar.activation(d[t][:], banks[PACK + t][:], COPY, scale=0.75)
+                d_n2 = keep.tile([P, HALF], F32, name="d_n2", tag="d_n2_%d" % t, align_bytes=64)
+                nc.scalar.activation(d_n2[:], d[t][:].indirect(n2_l[:, lcols[c]]), COPY)
+                nc.vector.tensor_tensor(first[c][:, t, :], d_n2[:], y[t][:, cols[c]], MULT)
 
-        w3_bf = weight_tiles("w3")
-        for c in range(2):
-            for u in range(2):
-                round_weight(False, w3_raw, w3_bf, c, u)
-        w3_q = [quantise_weight(w3_bf, u, "w3") for u in range(2)]
-
-        z_q = []
-        for c in range(2):
-            cols = slice(c * HALF, (c + 1) * HALF)
-            lcols = slice(c * LCOLS, (c + 1) * LCOLS)
-            first = keep.tile([P, PACK, HALF], F32, name="first%d" % c)
-            second = keep.tile([P, PACK, HALF], F32, name="second%d" % c)
-            for t in range(PACK):
-                y_n1 = keep.tile([P, HALF], F32, name="y_n1_%d_%d" % (c, t))
-                nc.scalar.activation(y_n1[:], y[t][:].indirect(n1_l[:, lcols]), COPY)
-                if c == 0:
-                    nc.vector.tensor_tensor(first[:, t, :], d[t][:].indirect(n2_l[:, lcols]), y[t][:, cols], MULT)
-                else:
-                    d_n2 = keep.tile([P, HALF], F32, name="d_n2_%d" % t)
-                    nc.scalar.activation(d_n2[:], d[t][:].indirect(n2_l[:, lcols]), COPY)
-                    nc.vector.tensor_tensor(first[:, t, :], d_n2[:], y[t][:, cols], MULT)
-                nc.vector.tensor_tensor(second[:, t, :], y_n1[:], d[t][:, cols], MULT)
-            z = keep.tile([P, HALF, PACK], BF16, name="z%d" % c, align_bytes=64)
+        def make_z(c, lo, hi, tag):
+            z = keep.tile([P, hi - lo, PACK], BF16, name="z", tag=tag, align_bytes=64)
             nc.vector.tensor_tensor(
                 z[:].rearrange("p (c e) t -> p c t e", e=2),
-                first[:].rearrange("p t (c e) -> p c t e", e=2),
-                second[:].rearrange("p t (c e) -> p c t e", e=2),
+                first[c][:, :, lo:hi].rearrange("p t (c e) -> p c t e", e=2),
+                second[c][:, :, lo:hi].rearrange("p t (c e) -> p c t e", e=2),
                 SUB,
             )
-            z_q.append(quantise(z[:].rearrange("p c t -> p (c t)"), "z%d" % c))
+            return z
+
+        def quantise_z(z, name):
+            return quantise(z[:].rearrange("p c t -> p (c t)"), name)
+
+        for t in range(2):
+            nc.scalar.activation(y[t][:], banks[t][:], COPY, scale=gain[:, t : t + 1])
+        nc.vector.tensor_scalar(y[2][:], banks[2][:], gain[:, 2:3], None, MULT)
+        fetched = fetch_y(0, 0)
+        nc.scalar.activation(y[3][:], banks[3][:], COPY, scale=gain[:, 3:4])
+        nc.vector.tensor_scalar(d[0][:], banks[PACK][:], 0.75, None, MULT)
+        for t in range(PACK):
+            if t > 0:
+                nc.scalar.activation(d[t][:], banks[PACK + t][:], COPY, scale=0.75)
+                fetched = fetch_y(0, t)
+            first_term(0, t, True)
+            second_term(0, t, fetched)
+        z_q = [quantise_z(make_z(0, 0, HALF, "z0"), "z0")]
+        w3_bf = [keep.tile([P, 2, P, PACK], BF16, name="w3_bf0", align_bytes=64)]
+        for c in range(2):
+            round_weight(False, w3_raw, w3_bf, c, 0)
+        w3_q = [quantise_weight(w3_bf, 0, "w3")]
+        for t in range(PACK):
+            second_term(1, t, fetch_y(1, t))
+        for t in range(PACK):
+            first_term(1, t, False)
+        z_tail = [make_z(1, 0, P, "z1"), make_z(1, P, HALF, "z2")]
+
+        z_q.extend([quantise_z(z_tail[0], "z1"), quantise_z(z_tail[1], "z2")])
+        w3_bf.append(keep.tile([P, 2, P, PACK], BF16, name="w3_bf1", tag="z1", align_bytes=64))
+        for c in range(2):
+            round_weight(False, w3_raw, w3_bf, c, 1)
+        w3_q.append(quantise_weight(w3_bf, 1, "w3"))
 
         out_rows = out.rearrange("(p t) c -> t p c", t=PACK)
-        for c in range(2):
-            for t in range(PACK):
-                product(banks[t][:, c * HALF : (c + 1) * HALF], w3_q, t, *z_q[c])
-        for t in range(PACK):
-            h = keep.tile([P, S], F32, name="h%d" % t)
-            nc.scalar.activation(h[:], banks[t][:], COPY)
+        h = [keep.tile([P, S], F32, name="h%d" % t) for t in range(PACK)]
+        spans = [slice(0, HALF), slice(HALF, HALF + P), slice(HALF + P, S)]
+        for i, span in enumerate(spans):
+            piece = banks[(0, 4, 5)[i]][:, span]
+            product(piece, w3_q, 0, *z_q[i])
+            nc.scalar.activation(h[0][:, span], piece, COPY)
+        for t in range(1, PACK):
+            for i, span in enumerate(spans):
+                product(banks[t][:, span], w3_q, t, *z_q[i])
+
+        pa = [keep.tile([P, W], F32, name="pa%d" % t) for t in range(PACK)]
+        nb = [keep.tile([P, W], F32, name="nb%d" % t) for t in range(PACK)]
+        res = [keep.tile([P, S], F32, name="res%d" % t) for t in range(PACK)]
+
+        def put_difference(t):
+            if t == 0:
+                nc.vector.tensor_copy(pa[t][:], h[t][:].indirect(n3_l[:]))
+            else:
+                nc.scalar.activation(h[t][:], banks[t][:], COPY)
+                nc.scalar.activation(pa[t][:], h[t][:].indirect(n3_l[:]), COPY)
+            nc.scalar.activation(nb[t][:], h[t][:].indirect(n4_l[:]), COPY, scale=-1.0)
+            nc.vector.tensor_tensor(res[t][:].indirect(n4_l[:]), pa[t][:], nb[t][:], ADD)
+
+        def put_sum(t):
             a75 = keep.tile([P, W], F32, name="a75_%d" % t)
             b75 = keep.tile([P, W], F32, name="b75_%d" % t)
-            pa = keep.tile([P, W], F32, name="pa%d" % t)
-            nb = keep.tile([P, W], F32, name="nb%d" % t)
-            res = keep.tile([P, S], F32, name="res%d" % t)
-            if t == 0:
-                nc.vector.tensor_copy(pa[:], h[:].indirect(n3_l[:]))
-            else:
-                nc.scalar.activation(pa[:], h[:].indirect(n3_l[:]), COPY)
-            nc.scalar.activation(nb[:], h[:].indirect(n4_l[:]), COPY, scale=-1.0)
-            nc.scalar.activation(a75[:], pa[:], COPY, scale=0.75)
-            nc.scalar.activation(b75[:], nb[:], COPY, scale=-0.75)
-            nc.vector.tensor_tensor(res[:].indirect(n4_l[:]), pa[:], nb[:], ADD)
-            nc.vector.tensor_tensor(res[:].indirect(n3_l[:]), a75[:], b75[:], ADD)
-            nc.sync.dma_start(out_rows[t], res[:])
+            nc.scalar.activation(a75[:], pa[t][:], COPY, scale=0.75)
+            nc.scalar.activation(b75[:], nb[t][:], COPY, scale=-0.75)
+            nc.vector.tensor_tensor(res[t][:].indirect(n3_l[:]), a75[:], b75[:], ADD)
+            nc.sync.dma_start(out_rows[t], res[t][:])
+
+        put_difference(0)
+        for t in range(1, PACK):
+            put_difference(t)
+            put_sum(t - 1)
+        put_sum(PACK - 1)

from contextlib import ExitStack

import concourse.mybir as mybir

K, T, S, N, H, W = 512, 2048, 512, 512, 512, 256
FLOPS = 2 * S * (2 * K * H + H * N)

F32 = mybir.dt.float32
BF16 = mybir.dt.bfloat16
I32 = mybir.dt.int32
U32 = mybir.dt.uint32
U16 = mybir.dt.uint16
U8 = mybir.dt.uint8
FP8X4 = mybir.dt.float8_e4m3fn_x4
COPY = mybir.ActivationFunctionType.Copy
MULT = mybir.AluOpType.mult
ADD = mybir.AluOpType.add
SUB = mybir.AluOpType.subtract

P = 128
PACK = 4
HALF = 256
LCOLS = HALF // 16


def tile_picked_twhcrossbhaar_none_p_kernel(
    tc, x_words, x_scales, w1, w2, gn, w3, offs, hz, n1, n2, n3, n4, out
):
    nc = tc.nc
    with ExitStack() as ctx:
        lists = ctx.enter_context(tc.tile_pool(name="lists", bufs=1))
        keep = ctx.enter_context(tc.tile_pool(name="keep", bufs=1))
        psum = ctx.enter_context(tc.psum_pool(name="psum", bufs=1))

        def load_list(src, name):
            tile = lists.tile(list(src.shape), U16, name=name)
            nc.sync.dma_start(tile[:], src)
            return tile

        def load_weight(w, tag):
            halves = []
            for c in range(2):
                raw = keep.tile([P, PACK, HALF], F32, name="raw", tag="%s%d" % (tag, c))
                nc.sync.dma_start(raw[:], w.rearrange("(p j) c -> p j c", j=PACK)[:, :, c * HALF : (c + 1) * HALF])
                halves.append(raw)
            return halves

        def weight_tiles(name):
            return [keep.tile([P, 2, P, PACK], BF16, name="%s_bf%d" % (name, u), align_bytes=64) for u in range(2)]

        def round_weight(on_scalar, raw, grouped, c, u):
            src = raw[c][:].rearrange("p j (m u e) -> p u m j e", u=2, e=2)[:, u]
            dst = grouped[u][:].rearrange("p e m j -> p m j e")[:, c * 64 : (c + 1) * 64]
            if on_scalar:
                nc.scalar.activation(dst, src, COPY)
            else:
                nc.vector.tensor_copy(dst, src)

        def quantise(src, name):
            width = src.shape[1] // PACK
            codes = keep.tile([P, width], U32, name=name + "_codes", align_bytes=64)
            scales = keep.tile([P, width], U8, name=name + "_scales", align_bytes=64)
            nc.vector.quantize_mx(out=codes[:].bitcast(FP8X4), scales=scales[:], in_=src)
            return codes, scales

        def quantise_weight(grouped, u, name):
            return quantise(grouped[u][:].rearrange("p e m j -> p (e m j)"), "%s_q%d" % (name, u))

        def product(dst, wq, t, codes, scales):
            w_codes, w_scales = wq[t // 2]
            cols = slice((t % 2) * P, (t % 2 + 1) * P)
            nc.tensor.matmul_mx(
                out=dst,
                lhsT=w_codes[:, cols].bitcast(FP8X4),
                lhsT_scale=w_scales[:, cols],
                rhs=codes[:].bitcast(FP8X4),
                rhs_scale=scales[:],
                start=True,
                stop=True,
            )

        scale_table = keep.tile([P, T], U8, name="scale_table", align_bytes=64)
        table_words = scale_table[:].bitcast(I32)
        scale_rows = x_scales[0].bitcast(I32)
        for q in range(4):
            nc.sync.dma_start(
                table_words[32 * q : 32 * (q + 1), :],
                scale_rows[4 * q : 4 * (q + 1), :].unsqueeze(0).broadcast_to([8, 4, T // 4]),
            )
        hz_l = load_list(hz, "hz_l")
        offs_l = load_list(offs, "offs_l")
        n1_l = load_list(n1, "n1_l")
        word_table = keep.tile([P, T], I32, name="word_table", align_bytes=64)
        nc.sync.dma_start(word_table[:], x_words[0].rearrange("p c r -> p (c r)").bitcast(I32))
        w1_raw = load_weight(w1, "w1_raw")
        w2_raw = load_weight(w2, "w2_raw")
        gain = keep.tile([P, PACK], F32, name="gain")
        nc.gpsimd.dma_start(gain[:], gn.rearrange("(p t) o -> p (t o)", t=PACK))

        hz_picked = keep.tile([P, S], U8, name="hz_picked", align_bytes=64)
        hz_scales = keep.tile([P, S], U8, name="hz_scales", align_bytes=64)
        x_scales_picked = keep.tile([P, S], U8, name="x_scales_picked", align_bytes=64)
        nc.vector.tensor_copy(hz_picked[:], scale_table[:].indirect(hz_l[:]))
        nc.vector.tensor_copy(x_scales_picked[:], scale_table[:].indirect(offs_l[:]))
        nc.vector.tensor_copy(hz_scales[:].bitcast(I32), hz_picked[:].bitcast(I32))
        for a in (2, 3):
            nc.sync.dma_start(hz_scales[:].bitcast(I32)[a:P:32, :], hz_picked[:].bitcast(I32)[16 + a : P : 32, :])
        n2_l = load_list(n2, "n2_l")
        w3_raw = load_weight(w3, "w3_raw")
        n3_l = load_list(n3, "n3_l")
        n4_l = load_list(n4, "n4_l")

        x_codes = keep.tile([P, S], U32, name="x_codes", align_bytes=64)
        hz_codes = keep.tile([P, S], U32, name="hz_codes", align_bytes=64)
        nc.vector.tensor_copy(x_codes[:], word_table[:].bitcast(U32).indirect(offs_l[:]))
        nc.vector.tensor_copy(hz_codes[:], word_table[:].bitcast(U32).indirect(hz_l[:]))

        w1_bf = weight_tiles("w1")
        for c in range(2):
            for u in range(2):
                round_weight(True, w1_raw, w1_bf, c, u)
        w1_q = [quantise_weight(w1_bf, u, "w1") for u in range(2)]

        banks = [psum.tile([P, S], F32, name="bank%d" % b) for b in range(8)]
        for t in range(PACK):
            product(banks[t][:], w1_q, t, x_codes, x_scales_picked)

        w2_bf = weight_tiles("w1")
        for c in range(2):
            for u in range(2):
                round_weight(False, w2_raw, w2_bf, c, u)
        w2_q = [quantise_weight(w2_bf, u, "w2") for u in range(2)]
        for t in range(PACK):
            product(banks[PACK + t][:], w2_q, t, hz_codes, hz_scales)

        y = [keep.tile([P, S], F32, name="y%d" % t) for t in range(PACK)]
        d = [keep.tile([P, S], F32, name="d%d" % t) for t in range(PACK)]

        first = [keep.tile([P, PACK, HALF], F32, name="first%d" % c) for c in range(2)]
        second = [keep.tile([P, PACK, HALF], F32, name="second%d" % c) for c in range(2)]
        cols = [slice(c * HALF, (c + 1) * HALF) for c in range(2)]
        lcols = [slice(c * LCOLS, (c + 1) * LCOLS) for c in range(2)]

        def fetch_y(c, t):
            y_n1 = keep.tile([P, HALF], F32, name="y_n1_%d_%d" % (c, t))
            nc.scalar.activation(y_n1[:], y[t][:].indirect(n1_l[:, lcols[c]]), COPY)
            return y_n1

        def second_term(c, t, y_n1):
            nc.vector.tensor_tensor(second[c][:, t, :], y_n1[:], d[t][:, cols[c]], MULT)

        def first_term(c, t, fused):
            if fused:
                nc.vector.tensor_tensor(first[c][:, t, :], d[t][:].indirect(n2_l[:, lcols[c]]), y[t][:, cols[c]], MULT)
            else:
                d_n2 = keep.tile([P, HALF], F32, name="d_n2", tag="d_n2_%d" % t, align_bytes=64)
                nc.scalar.activation(d_n2[:], d[t][:].indirect(n2_l[:, lcols[c]]), COPY)
                nc.vector.tensor_tensor(first[c][:, t, :], d_n2[:], y[t][:, cols[c]], MULT)

        def make_z(c, lo, hi, tag):
            z = keep.tile([P, hi - lo, PACK], BF16, name="z", tag=tag, align_bytes=64)
            nc.vector.tensor_tensor(
                z[:].rearrange("p (c e) t -> p c t e", e=2),
                first[c][:, :, lo:hi].rearrange("p t (c e) -> p c t e", e=2),
                second[c][:, :, lo:hi].rearrange("p t (c e) -> p c t e", e=2),
                SUB,
            )
            return z

        def quantise_z(z, name):
            return quantise(z[:].rearrange("p c t -> p (c t)"), name)

        for t in range(2):
            nc.scalar.activation(y[t][:], banks[t][:], COPY, scale=gain[:, t : t + 1])
        nc.vector.tensor_scalar(y[2][:], banks[2][:], gain[:, 2:3], None, MULT)
        fetched = fetch_y(0, 0)
        nc.scalar.activation(y[3][:], banks[3][:], COPY, scale=gain[:, 3:4])
        nc.vector.tensor_scalar(d[0][:], banks[PACK][:], 0.75, None, MULT)
        for t in range(PACK):
            if t > 0:
                nc.scalar.activation(d[t][:], banks[PACK + t][:], COPY, scale=0.75)
                fetched = fetch_y(0, t)
            first_term(0, t, True)
            second_term(0, t, fetched)
        z_q = [quantise_z(make_z(0, 0, HALF, "z0"), "z0")]
        w3_bf = [keep.tile([P, 2, P, PACK], BF16, name="w3_bf0", align_bytes=64)]
        for c in range(2):
            round_weight(False, w3_raw, w3_bf, c, 0)
        w3_q = [quantise_weight(w3_bf, 0, "w3")]
        for t in range(PACK):
            second_term(1, t, fetch_y(1, t))
        for t in range(PACK):
            first_term(1, t, False)
        z_tail = [make_z(1, 0, P, "z1"), make_z(1, P, HALF, "z2")]

        z_q.extend([quantise_z(z_tail[0], "z1"), quantise_z(z_tail[1], "z2")])
        w3_bf.append(keep.tile([P, 2, P, PACK], BF16, name="w3_bf1", tag="z1", align_bytes=64))
        for c in range(2):
            round_weight(False, w3_raw, w3_bf, c, 1)
        w3_q.append(quantise_weight(w3_bf, 1, "w3"))

        out_rows = out.rearrange("(p t) c -> t p c", t=PACK)
        h = [keep.tile([P, S], F32, name="h%d" % t) for t in range(PACK)]
        spans = [slice(0, HALF), slice(HALF, HALF + P), slice(HALF + P, S)]
        for i, span in enumerate(spans):
            piece = banks[(0, 4, 5)[i]][:, span]
            product(piece, w3_q, 0, *z_q[i])
            nc.scalar.activation(h[0][:, span], piece, COPY)
        for t in range(1, PACK):
            for i, span in enumerate(spans):
                product(banks[t][:, span], w3_q, t, *z_q[i])

        pa = [keep.tile([P, W], F32, name="pa%d" % t) for t in range(PACK)]
        nb = [keep.tile([P, W], F32, name="nb%d" % t) for t in range(PACK)]
        res = [keep.tile([P, S], F32, name="res%d" % t) for t in range(PACK)]

        def put_difference(t):
            if t == 0:
                nc.vector.tensor_copy(pa[t][:], h[t][:].indirect(n3_l[:]))
            else:
                nc.scalar.activation(h[t][:], banks[t][:], COPY)
                nc.scalar.activation(pa[t][:], h[t][:].indirect(n3_l[:]), COPY)
            nc.scalar.activation(nb[t][:], h[t][:].indirect(n4_l[:]), COPY, scale=-1.0)
            nc.vector.tensor_tensor(res[t][:].indirect(n4_l[:]), pa[t][:], nb[t][:], ADD)

        def put_sum(t):
            a75 = keep.tile([P, W], F32, name="a75_%d" % t)
            b75 = keep.tile([P, W], F32, name="b75_%d" % t)
            nc.scalar.activation(a75[:], pa[t][:], COPY, scale=0.75)
            nc.scalar.activation(b75[:], nb[t][:], COPY, scale=-0.75)
            nc.vector.tensor_tensor(res[t][:].indirect(n3_l[:]), a75[:], b75[:], ADD)
            nc.sync.dma_start(out_rows[t], res[t][:])

        put_difference(0)
        for t in range(1, PACK):
            put_difference(t)
            put_sum(t - 1)
        put_sum(PACK - 1)
